import numpy as np
import ml_dtypes


def mxq(x, axis, fmt="e4m3"):
    dtype, down = {"e4m3": (ml_dtypes.float8_e4m3fn, 7), "e5m2": (ml_dtypes.float8_e5m2, 14)}[fmt]
    v = np.moveaxis(np.asarray(x, np.float32).astype(ml_dtypes.bfloat16).astype(np.float64), axis, -1)
    blocks = v.reshape(v.shape[:-1] + (-1, 32))
    amax = np.abs(blocks).max(-1, keepdims=True)
    byte = np.maximum(np.where(amax > 0, np.frexp(amax)[1] - 1 + 127, 0) - down, 1)
    scale = np.exp2(byte - 127.0)
    codes = (blocks / scale).astype(np.float32).astype(dtype).astype(np.float64)
    return np.moveaxis((codes * scale).reshape(v.shape), -1, axis)


WIDE = False


def mx_kscale(k):
    if not WIDE:
        return np.ones(k)
    levels = np.array([10, -10, 5, -5, 0])
    if k % 512:
        return np.exp2(np.random.permutation(np.resize(levels, k // 32))).repeat(32)
    a = np.empty((k // 512, 16))
    for p in range(k // 512):
        a[p, :8] = np.random.permutation(np.resize(levels, 8))
        for g in range(8):
            far = levels[np.abs(levels - a[p, g]) >= 10]
            a[p, g + 8] = far[np.random.randint(len(far))]
    return np.exp2(a.ravel()).repeat(32)


def f64(x):
    return np.asarray(x).astype(np.float64)


def striped(idx):
    return np.tile(np.asarray(idx).reshape(-1, 16).T, (8, 1)).astype(np.uint16)


def unstriped(offs):
    return offs[:16].T.reshape(-1).astype(np.int64)


E2M1 = np.array([0.0, 0.5, 1.0, 1.5, 2.0, 3.0, 4.0, 6.0, -0.0, -0.5, -1.0, -1.5, -2.0, -3.0, -4.0, -6.0])


def pack_weight(w, fmt):
    k, n = w.shape
    w = f64(np.asarray(w, np.float32).astype(ml_dtypes.bfloat16)).reshape(k // 32, 32, n)
    amax = np.abs(w).max(1)
    if fmt == "e4m3":
        byte = np.frexp(amax)[1] - 1 + 127 - 7
    else:
        mant, ex = np.frexp(amax / 6.0)
        byte = np.where(mant > 0.5, ex, ex - 1) + 127
    byte = np.clip(np.where(amax > 0, byte, 1), 1, 254)
    scaled = (w * np.exp2(127.0 - byte)[:, None, :]).reshape(k, n).astype(np.float32)
    by_word = np.ascontiguousarray(scaled.reshape(k // 512, 128, 4, n).transpose(0, 1, 3, 2))
    if fmt == "e4m3":
        words = by_word.astype(ml_dtypes.float8_e4m3fn).view(np.uint8)
    else:
        c = by_word.astype(ml_dtypes.float4_e2m1fn).view(np.uint8) & 0xF
        words = (c[..., 0::2] | (c[..., 1::2] << 4)).reshape(k // 512, 128, 2 * n)
    return np.ascontiguousarray(words), np.ascontiguousarray(byte.astype(np.uint8).reshape(k // 512, 16, n))


def unpack_weight(words, scales, fmt):
    g, _, n = scales.shape
    words = np.ascontiguousarray(words).reshape(g, 128, n, -1)
    if fmt == "e4m3":
        vals = words.view(ml_dtypes.float8_e4m3fn).astype(np.float64)
    else:
        nib = np.empty((g, 128, n, 4), np.uint8)
        nib[..., 0::2] = words & 0xF
        nib[..., 1::2] = words >> 4
        vals = E2M1[nib]
    vals = vals * np.repeat(np.exp2(scales.astype(np.float64) - 127.0), 8, axis=1)[..., None]
    return vals.transpose(0, 1, 3, 2).reshape(g * 512, n)


def softplus(v):
    return np.log(1.0 + np.exp(v))


D, T, I, Q = 512, 2048, 512, 128


def setup_inputs():
    n = np.random.standard_normal
    idx = np.random.permutation(T)[:I]
    fd = mx_kscale(D)
    keysp = pack_weight(n((D, T)) / fd[:, None], "e2m1")
    return {
        "query": (n((D, Q)) * 1.0 / np.sqrt(D) * fd[:, None]).astype(np.float32),
        "keys_words": keysp[0],
        "keys_scales": keysp[1],
        "margin": (np.random.uniform(0.0, 0.5, (1, I))).astype(np.float32),
        "steep": (np.random.uniform(0.5, 2.0, (Q, 1))).astype(np.float32),
        "offs": striped(idx),
    }


def reference(query, keys_words, keys_scales, margin, steep, offs):
    idx = unstriped(offs)
    keysu = unpack_weight(keys_words, keys_scales, "e2m1")
    queryq = mxq(f64(query), 0, "e4m3")
    keysidxg = keysu[:, idx]
    a = queryq.T @ keysidxg
    b = np.pad(a, ((0, 0), (1, 0)))[:, :I]
    y = softplus((a - b + f64(margin)) * f64(steep))
    return y

@@ -1,0 +1,167 @@
+import math
+from contextlib import ExitStack
+
+import concourse.mybir as mybir
+from concourse.masks import make_identity
+
+D, T, I, Q = 512, 2048, 512, 128
+FLOPS = 2 * D * I * Q
+
+F32 = mybir.dt.float32
+BF16 = mybir.dt.bfloat16
+I32 = mybir.dt.int32
+U32 = mybir.dt.uint32
+U16 = mybir.dt.uint16
+U8 = mybir.dt.uint8
+FP8X4 = mybir.dt.float8_e4m3fn_x4
+FP4X4 = mybir.dt.float4_e2m1fn_x4
+ALU = mybir.AluOpType
+ACT = mybir.ActivationFunctionType
+
+P = 128
+PACK = 4
+HALF = I // 2
+
+
+def det3(m):
+    return (
+        m[0][0] * (m[1][1] * m[2][2] - m[1][2] * m[2][1])
+        - m[0][1] * (m[1][0] * m[2][2] - m[1][2] * m[2][0])
+        + m[0][2] * (m[1][0] * m[2][1] - m[1][1] * m[2][0])
+    )
+
+
+def log1p_terms():
+    root2 = math.sqrt(2.0)
+    reach = (root2 - 1.0) / (root2 + 1.0)
+    rows, rhs = [], []
+    for node in range(3):
+        z = reach * math.cos((2 * node + 1) * math.pi / 14)
+        g = math.log((1.0 + z) / (1.0 - z)) / z
+        rows.append([g, -1.0, z * z])
+        rhs.append(g * z * z)
+    pole2, joint, slope = [
+        det3([[rhs[r] if c == col else rows[r][c] for c in range(3)] for r in range(3)]) / det3(rows)
+        for col in range(3)
+    ]
+    spread = joint - slope * pole2
+    centre = 1.0 + root2
+    terms = [(-root2 * slope / centre, math.log(centre))]
+    for z0 in (math.sqrt(pole2), -math.sqrt(pole2)):
+        place = 1.0 - root2 * (1.0 + z0) / (1.0 - z0)
+        terms.append((-0.25 * spread * (centre - place) / ((1.0 - z0) * place), math.log(place)))
+    at_zero = math.log(root2) - reach * (slope + spread / (pole2 - reach * reach))
+    return at_zero - sum(w for w, s in terms), terms
+
+
+def tile_attend_rankgaps_kernel(tc, query, keys_words, keys_scales, margin, steep, offs, out):
+    nc = tc.nc
+    level, terms = log1p_terms()
+    with ExitStack() as ctx:
+        keep = ctx.enter_context(tc.tile_pool(name="keep", bufs=1))
+        psum = ctx.enter_context(tc.psum_pool(name="psum", bufs=1))
+
+        offsets = keep.tile([P, I // 16], U16, name="offsets")
+        store_scales = keep.tile([P, T], U8, name="store_scales", align_bytes=64)
+        store_words = keep.tile([P, T], U16, name="store_words", align_bytes=64)
+        query_raw = keep.tile([P, PACK, Q], F32, name="query_raw")
+        margin_col = keep.tile([P, PACK], F32, name="margin_col")
+        steep_col = keep.tile([P, 1], F32, name="steep_col")
+
+        nc.vector.memset(store_scales[:].bitcast(I32), 0)
+        nc.scalar.dma_start(out=margin_col[:], in_=margin.rearrange("o (p c) -> (o p) c", c=PACK))
+        nc.sync.dma_start(offsets[:], offs)
+        for quad in range(4):
+            nc.sync.dma_start(
+                out=store_scales[32 * quad : 32 * quad + 4, :].bitcast(I32),
+                in_=keys_scales[0, 4 * quad : 4 * quad + 4, :].bitcast(I32),
+            )
+        nc.scalar.dma_start(out=query_raw[:], in_=query.rearrange("(p j) q -> p j q", j=PACK))
+        nc.scalar.dma_start(out=store_words[:].bitcast(I32), in_=keys_words[0].bitcast(I32))
+        ident = keep.tile([P, P], F32, name="ident")
+        nc.vector.memset(ident[:], 0.0)
+        make_identity(nc, ident[:], nomemset=True)
+        nc.gpsimd.dma_start(out=steep_col[:], in_=steep)
+
+        picked_scales = keep.tile([P, I], U8, name="picked_scales", align_bytes=64)
+        nc.vector.tensor_copy(picked_scales[:], store_scales[:].indirect(offsets[:]))
+
+        query_bf = keep.tile([P, Q, PACK], BF16, name="query_bf", tag="picked_words0", align_bytes=64)
+        nc.scalar.activation(query_bf[:], query_raw[:].rearrange("p j q -> p q j"), ACT.Copy)
+        query_codes = keep.tile([P, Q], U32, name="query_codes", align_bytes=64)
+        query_scales = keep.tile([P, Q], U8, name="query_scales", align_bytes=64)
+        nc.vector.quantize_mx(
+            out=query_codes[:].bitcast(FP8X4),
+            scales=query_scales[:],
+            in_=query_bf[:].rearrange("p q j -> p (q j)"),
+        )
+
+        margin_bank = psum.tile([P, PACK, P], F32, name="margin_bank", tag="banks")
+        for c in range(PACK):
+            nc.tensor.transpose(margin_bank[:, c, :], margin_col[:, c : c + 1].to_broadcast([P, P]), ident[:])
+        steep_neg = keep.tile([P, 1], F32, name="steep_neg")
+        nc.scalar.activation(steep_neg[:], steep_col[:], ACT.Copy, scale=-1.0)
+        behind = keep.tile([P, I], F32, name="behind")
+        nc.scalar.activation(
+            behind[:].rearrange("q (p c) -> q p c", c=PACK),
+            margin_bank[:].rearrange("q c p -> q p c"),
+            ACT.Copy,
+            scale=steep_neg[:],
+        )
+
+        banks = []
+        scores = psum.tile([P, 2, 512], F32, name="scores", tag="banks")
+        for half in range(2):
+            words = keep.tile([P, HALF], U16, name=f"picked_words{half}", tag=f"picked_words{half}", align_bytes=64)
+            cols = slice(half * HALF // 16, (half + 1) * HALF // 16)
+            nc.vector.tensor_copy(words[:], store_words[:].indirect(offsets[:, cols]))
+            bank = scores[:, half, :HALF]
+            nc.tensor.matmul_mx(
+                out=bank,
+                lhsT=query_codes[:].bitcast(FP8X4),
+                lhsT_scale=query_scales[:],
+                rhs=words[:].bitcast(FP4X4),
+                rhs_scale=picked_scales[:, half * HALF : (half + 1) * HALF],
+                start=True,
+                stop=True,
+            )
+            banks.append(bank)
+
+        gap = keep.tile([P, I], F32, name="gap")
+        size = keep.tile([P, I], F32, name="size")
+        bends = [keep.tile([P, I], F32, name=f"bend{j}") for j in range(3)]
+        sums = [keep.tile([P, I], F32, name=f"sum{j}") for j in range(4)]
+        chunks = [(0, 256), (256, 512)]
+
+        def shift(lo, hi):
+            bank = banks[lo // HALF]
+            base = lo // HALF * HALF
+            end = min(hi, I - 1)
+            nc.vector.scalar_tensor_tensor(
+                behind[:, lo + 1 : end + 1], bank[:, lo - base : end - base], steep_col[:],
+                behind[:, lo + 1 : end + 1], ALU.mult, ALU.add,
+            )
+
+        def diff(lo, hi):
+            bank = banks[lo // HALF]
+            base = lo // HALF * HALF
+            nc.vector.scalar_tensor_tensor(
+                gap[:, lo:hi], bank[:, lo - base : hi - base], steep_col[:],
+                behind[:, lo:hi], ALU.mult, ALU.subtract,
+            )
+
+        for lo, hi in chunks:
+            shift(lo, hi)
+        for lo, hi in chunks:
+            diff(lo, hi)
+        for lo, hi in chunks:
+            nc.scalar.activation(size[:, lo:hi], gap[:, lo:hi], ACT.Abs)
+            nc.vector.tensor_scalar(sums[0][:, lo:hi], gap[:, lo:hi], 0.0, level, ALU.max, ALU.add)
+        for j, (weight, place) in enumerate(terms):
+            for lo, hi in chunks:
+                nc.scalar.activation(bends[j][:, lo:hi], size[:, lo:hi], ACT.Tanh, bias=0.5 * place, scale=0.5)
+                nc.vector.scalar_tensor_tensor(
+                    sums[j + 1][:, lo:hi], bends[j][:, lo:hi], weight, sums[j][:, lo:hi], ALU.mult, ALU.add
+                )
+        for lo, hi in chunks:
+            nc.sync.dma_start(out=out[:, lo:hi], in_=sums[3][:, lo:hi])

@@ -64,44 +64,37 @@ def tile_attend_rankgaps_kernel(tc, query, keys_words, keys_scales, margin, stee
         offsets = keep.tile([P, I // 16], U16, name="offsets")
         store_scales = keep.tile([P, T], U8, name="store_scales", align_bytes=64)
         store_words = keep.tile([P, T], U16, name="store_words", align_bytes=64)
-        query_raw = keep.tile([P, PACK, Q], F32, name="query_raw")
+        query_raw = keep.tile([P, PACK, Q], F32, name="query_raw", tag="behind")
         margin_col = keep.tile([P, PACK], F32, name="margin_col")
         steep_col = keep.tile([P, 1], F32, name="steep_col")
 
         nc.vector.memset(store_scales[:].bitcast(I32), 0)
-        nc.scalar.dma_start(out=margin_col[:], in_=margin.rearrange("o (p c) -> (o p) c", c=PACK))
         nc.sync.dma_start(offsets[:], offs)
+        nc.sync.dma_start(out=store_words[:].bitcast(I32), in_=keys_words[0].bitcast(I32))
+        nc.sync.dma_start(out=query_raw[:], in_=query.rearrange("(p j) q -> p j q", j=PACK))
+        nc.scalar.dma_start(out=margin_col[:], in_=margin.rearrange("o (p c) -> (o p) c", c=PACK))
+        nc.scalar.dma_start(out=steep_col[:], in_=steep)
         for quad in range(4):
             nc.sync.dma_start(
                 out=store_scales[32 * quad : 32 * quad + 4, :].bitcast(I32),
                 in_=keys_scales[0, 4 * quad : 4 * quad + 4, :].bitcast(I32),
             )
-        nc.scalar.dma_start(out=query_raw[:], in_=query.rearrange("(p j) q -> p j q", j=PACK))
-        nc.scalar.dma_start(out=store_words[:].bitcast(I32), in_=keys_words[0].bitcast(I32))
-        ident = keep.tile([P, P], F32, name="ident")
+        ident = keep.tile([P, P], F32, name="ident", tag="query_codes", align_bytes=64)
         nc.vector.memset(ident[:], 0.0)
         make_identity(nc, ident[:], nomemset=True)
-        nc.gpsimd.dma_start(out=steep_col[:], in_=steep)
 
-        picked_scales = keep.tile([P, I], U8, name="picked_scales", align_bytes=64)
-        nc.vector.tensor_copy(picked_scales[:], store_scales[:].indirect(offsets[:]))
+        picked_words = keep.tile([P, I], U16, name="picked_words", align_bytes=64)
+        nc.vector.tensor_copy(picked_words[:], store_words[:].indirect(offsets[:]))
 
-        query_bf = keep.tile([P, Q, PACK], BF16, name="query_bf", tag="picked_words0", align_bytes=64)
+        query_bf = keep.tile([P, Q, PACK], BF16, name="query_bf", tag="picked_scales", align_bytes=64)
         nc.scalar.activation(query_bf[:], query_raw[:].rearrange("p j q -> p q j"), ACT.Copy)
-        query_codes = keep.tile([P, Q], U32, name="query_codes", align_bytes=64)
-        query_scales = keep.tile([P, Q], U8, name="query_scales", align_bytes=64)
-        nc.vector.quantize_mx(
-            out=query_codes[:].bitcast(FP8X4),
-            scales=query_scales[:],
-            in_=query_bf[:].rearrange("p q j -> p (q j)"),
-        )
 
-        margin_bank = psum.tile([P, PACK, P], F32, name="margin_bank", tag="banks")
+        margin_bank = psum.tile([P, PACK, P], F32, name="margin_bank")
         for c in range(PACK):
             nc.tensor.transpose(margin_bank[:, c, :], margin_col[:, c : c + 1].to_broadcast([P, P]), ident[:])
         steep_neg = keep.tile([P, 1], F32, name="steep_neg")
         nc.scalar.activation(steep_neg[:], steep_col[:], ACT.Copy, scale=-1.0)
-        behind = keep.tile([P, I], F32, name="behind")
+        behind = keep.tile([P, I], F32, name="behind", tag="behind")
         nc.scalar.activation(
             behind[:].rearrange("q (p c) -> q p c", c=PACK),
             margin_bank[:].rearrange("q c p -> q p c"),
@@ -109,19 +102,27 @@ def tile_attend_rankgaps_kernel(tc, query, keys_words, keys_scales, margin, stee
             scale=steep_neg[:],
         )
 
+        query_codes = keep.tile([P, Q], U32, name="query_codes", tag="query_codes", align_bytes=64)
+        query_scales = keep.tile([P, Q], U8, name="query_scales", align_bytes=64)
+        nc.vector.quantize_mx(
+            out=query_codes[:].bitcast(FP8X4),
+            scales=query_scales[:],
+            in_=query_bf[:].rearrange("p q j -> p (q j)"),
+        )
+
         banks = []
-        scores = psum.tile([P, 2, 512], F32, name="scores", tag="banks")
+        picked_scales = keep.tile([P, I], U8, name="picked_scales", tag="picked_scales", align_bytes=64)
         for half in range(2):
-            words = keep.tile([P, HALF], U16, name=f"picked_words{half}", tag=f"picked_words{half}", align_bytes=64)
+            slots = slice(half * HALF, (half + 1) * HALF)
             cols = slice(half * HALF // 16, (half + 1) * HALF // 16)
-            nc.vector.tensor_copy(words[:], store_words[:].indirect(offsets[:, cols]))
-            bank = scores[:, half, :HALF]
+            nc.vector.tensor_copy(picked_scales[:, slots], store_scales[:].indirect(offsets[:, cols]))
+            bank = psum.tile([P, HALF], F32, name=f"score_bank{half}")
             nc.tensor.matmul_mx(
-                out=bank,
+                out=bank[:],
                 lhsT=query_codes[:].bitcast(FP8X4),
                 lhsT_scale=query_scales[:],
-                rhs=words[:].bitcast(FP4X4),
-                rhs_scale=picked_scales[:, half * HALF : (half + 1) * HALF],
+                rhs=picked_words[:, slots].bitcast(FP4X4),
+                rhs_scale=picked_scales[:, slots],
                 start=True,
                 stop=True,
             )

@@ -73,7 +73,7 @@ def tile_attend_rankgaps_kernel(tc, query, keys_words, keys_scales, margin, stee
         nc.sync.dma_start(out=store_words[:].bitcast(I32), in_=keys_words[0].bitcast(I32))
         nc.sync.dma_start(out=query_raw[:], in_=query.rearrange("(p j) q -> p j q", j=PACK))
         nc.scalar.dma_start(out=margin_col[:], in_=margin.rearrange("o (p c) -> (o p) c", c=PACK))
-        nc.scalar.dma_start(out=steep_col[:], in_=steep)
+        nc.gpsimd.dma_start(out=steep_col[:], in_=steep)
         for quad in range(4):
             nc.sync.dma_start(
                 out=store_scales[32 * quad : 32 * quad + 4, :].bitcast(I32),
@@ -86,22 +86,30 @@ def tile_attend_rankgaps_kernel(tc, query, keys_words, keys_scales, margin, stee
         picked_words = keep.tile([P, I], U16, name="picked_words", align_bytes=64)
         nc.vector.tensor_copy(picked_words[:], store_words[:].indirect(offsets[:]))
 
-        query_bf = keep.tile([P, Q, PACK], BF16, name="query_bf", tag="picked_scales", align_bytes=64)
+        query_bf = keep.tile([P, Q, PACK], BF16, name="query_bf", tag="picked_scales1", align_bytes=64)
         nc.scalar.activation(query_bf[:], query_raw[:].rearrange("p j q -> p q j"), ACT.Copy)
 
         margin_bank = psum.tile([P, PACK, P], F32, name="margin_bank")
         for c in range(PACK):
             nc.tensor.transpose(margin_bank[:, c, :], margin_col[:, c : c + 1].to_broadcast([P, P]), ident[:])
-        steep_neg = keep.tile([P, 1], F32, name="steep_neg")
-        nc.scalar.activation(steep_neg[:], steep_col[:], ACT.Copy, scale=-1.0)
         behind = keep.tile([P, I], F32, name="behind", tag="behind")
         nc.scalar.activation(
             behind[:].rearrange("q (p c) -> q p c", c=PACK),
             margin_bank[:].rearrange("q c p -> q p c"),
             ACT.Copy,
-            scale=steep_neg[:],
+            scale=steep_col[:],
         )
+        nc.scalar.activation(behind[:, 0:1], behind[:, 0:1], ACT.Copy, scale=-1.0)
 
+        picked_scales = []
+
+        def gather_scales(half):
+            tile = keep.tile([P, HALF], U8, name=f"picked_scales{half}", tag=f"picked_scales{half}", align_bytes=64)
+            cols = slice(half * HALF // 16, (half + 1) * HALF // 16)
+            nc.vector.tensor_copy(tile[:], store_scales[:].indirect(offsets[:, cols]))
+            picked_scales.append(tile)
+
+        gather_scales(0)
         query_codes = keep.tile([P, Q], U32, name="query_codes", tag="query_codes", align_bytes=64)
         query_scales = keep.tile([P, Q], U8, name="query_scales", align_bytes=64)
         nc.vector.quantize_mx(
@@ -109,20 +117,17 @@ def tile_attend_rankgaps_kernel(tc, query, keys_words, keys_scales, margin, stee
             scales=query_scales[:],
             in_=query_bf[:].rearrange("p q j -> p (q j)"),
         )
+        gather_scales(1)
 
         banks = []
-        picked_scales = keep.tile([P, I], U8, name="picked_scales", tag="picked_scales", align_bytes=64)
         for half in range(2):
-            slots = slice(half * HALF, (half + 1) * HALF)
-            cols = slice(half * HALF // 16, (half + 1) * HALF // 16)
-            nc.vector.tensor_copy(picked_scales[:, slots], store_scales[:].indirect(offsets[:, cols]))
             bank = psum.tile([P, HALF], F32, name=f"score_bank{half}")
             nc.tensor.matmul_mx(
                 out=bank[:],
                 lhsT=query_codes[:].bitcast(FP8X4),
                 lhsT_scale=query_scales[:],
-                rhs=picked_words[:, slots].bitcast(FP4X4),
-                rhs_scale=picked_scales[:, slots],
+                rhs=picked_words[:, half * HALF : (half + 1) * HALF].bitcast(FP4X4),
+                rhs_scale=picked_scales[half][:],
                 start=True,
                 stop=True,
             )
@@ -140,7 +145,7 @@ def tile_attend_rankgaps_kernel(tc, query, keys_words, keys_scales, margin, stee
             end = min(hi, I - 1)
             nc.vector.scalar_tensor_tensor(
                 behind[:, lo + 1 : end + 1], bank[:, lo - base : end - base], steep_col[:],
-                behind[:, lo + 1 : end + 1], ALU.mult, ALU.add,
+                behind[:, lo + 1 : end + 1], ALU.mult, ALU.subtract,
             )
 
         def diff(lo, hi):

@@ -2,7 +2,6 @@ import math
 from contextlib import ExitStack
 
 import concourse.mybir as mybir
-from concourse.masks import make_identity
 
 D, T, I, Q = 512, 2048, 512, 128
 FLOPS = 2 * D * I * Q
@@ -66,22 +65,32 @@ def tile_attend_rankgaps_kernel(tc, query, keys_words, keys_scales, margin, stee
         store_words = keep.tile([P, T], U16, name="store_words", align_bytes=64)
         query_raw = keep.tile([P, PACK, Q], F32, name="query_raw", tag="behind")
         margin_col = keep.tile([P, PACK], F32, name="margin_col")
-        steep_col = keep.tile([P, 1], F32, name="steep_col")
 
         nc.vector.memset(store_scales[:].bitcast(I32), 0)
+        zeros = keep.tile([P, P], F32, name="zeros", tag="steep_col")
+        nc.vector.memset(zeros[:], 0.0)
+        ident = keep.tile([P, P], F32, name="ident", tag="query_codes", align_bytes=64)
+        nc.gpsimd.affine_select(
+            out=ident[:],
+            in_=zeros[:],
+            compare_op=ALU.not_equal,
+            fill=1.0,
+            base=0,
+            pattern=[[-1, P]],
+            channel_multiplier=1,
+        )
+
         nc.sync.dma_start(offsets[:], offs)
         nc.sync.dma_start(out=store_words[:].bitcast(I32), in_=keys_words[0].bitcast(I32))
         nc.sync.dma_start(out=query_raw[:], in_=query.rearrange("(p j) q -> p j q", j=PACK))
         nc.scalar.dma_start(out=margin_col[:], in_=margin.rearrange("o (p c) -> (o p) c", c=PACK))
-        nc.gpsimd.dma_start(out=steep_col[:], in_=steep)
-        for quad in range(4):
+        for row in range(4):
             nc.sync.dma_start(
-                out=store_scales[32 * quad : 32 * quad + 4, :].bitcast(I32),
-                in_=keys_scales[0, 4 * quad : 4 * quad + 4, :].bitcast(I32),
+                out=store_scales[row:P:32, :].bitcast(I32),
+                in_=keys_scales[0, row:16:4, :].bitcast(I32),
             )
-        ident = keep.tile([P, P], F32, name="ident", tag="query_codes", align_bytes=64)
-        nc.vector.memset(ident[:], 0.0)
-        make_identity(nc, ident[:], nomemset=True)
+        steep_col = keep.tile([P, 1], F32, name="steep_col", tag="steep_col")
+        nc.sync.dma_start(out=steep_col[:], in_=steep)
 
         picked_words = keep.tile([P, I], U16, name="picked_words", align_bytes=64)
         nc.vector.tensor_copy(picked_words[:], store_words[:].indirect(offsets[:]))
@@ -101,13 +110,14 @@ def tile_attend_rankgaps_kernel(tc, query, keys_words, keys_scales, margin, stee
         )
         nc.scalar.activation(behind[:, 0:1], behind[:, 0:1], ACT.Copy, scale=-1.0)
 
-        picked_scales = []
+        picked_scales = [
+            keep.tile([P, HALF], U8, name=f"picked_scales{half}", tag=f"picked_scales{half}", align_bytes=64)
+            for half in range(2)
+        ]
 
         def gather_scales(half):
-            tile = keep.tile([P, HALF], U8, name=f"picked_scales{half}", tag=f"picked_scales{half}", align_bytes=64)
             cols = slice(half * HALF // 16, (half + 1) * HALF // 16)
-            nc.vector.tensor_copy(tile[:], store_scales[:].indirect(offsets[:, cols]))
-            picked_scales.append(tile)
+            nc.vector.tensor_copy(picked_scales[half][:], store_scales[:].indirect(offsets[:, cols]))
 
         gather_scales(0)
         query_codes = keep.tile([P, Q], U32, name="query_codes", tag="query_codes", align_bytes=64)

@@ -81,11 +81,11 @@ def tile_attend_rankgaps_kernel(tc, query, keys_words, keys_scales, margin, stee
         )
 
         nc.sync.dma_start(offsets[:], offs)
-        nc.sync.dma_start(out=store_words[:].bitcast(I32), in_=keys_words[0].bitcast(I32))
-        nc.sync.dma_start(out=query_raw[:], in_=query.rearrange("(p j) q -> p j q", j=PACK))
-        nc.scalar.dma_start(out=margin_col[:], in_=margin.rearrange("o (p c) -> (o p) c", c=PACK))
+        nc.scalar.dma_start(out=store_words[:].bitcast(I32), in_=keys_words[0].bitcast(I32))
+        nc.scalar.dma_start(out=query_raw[:], in_=query.rearrange("(p j) q -> p j q", j=PACK))
+        nc.sync.dma_start(out=margin_col[:], in_=margin.rearrange("o (p c) -> (o p) c", c=PACK))
         for row in range(4):
-            nc.sync.dma_start(
+            nc.scalar.dma_start(
                 out=store_scales[row:P:32, :].bitcast(I32),
                 in_=keys_scales[0, row:16:4, :].bitcast(I32),
             )

import math
from contextlib import ExitStack

import concourse.mybir as mybir

D, T, I, Q = 512, 2048, 512, 128
FLOPS = 2 * D * I * Q

F32 = mybir.dt.float32
BF16 = mybir.dt.bfloat16
I32 = mybir.dt.int32
U32 = mybir.dt.uint32
U16 = mybir.dt.uint16
U8 = mybir.dt.uint8
FP8X4 = mybir.dt.float8_e4m3fn_x4
FP4X4 = mybir.dt.float4_e2m1fn_x4
ALU = mybir.AluOpType
ACT = mybir.ActivationFunctionType

P = 128
PACK = 4
HALF = I // 2


def det3(m):
    return (
        m[0][0] * (m[1][1] * m[2][2] - m[1][2] * m[2][1])
        - m[0][1] * (m[1][0] * m[2][2] - m[1][2] * m[2][0])
        + m[0][2] * (m[1][0] * m[2][1] - m[1][1] * m[2][0])
    )


def log1p_terms():
    root2 = math.sqrt(2.0)
    reach = (root2 - 1.0) / (root2 + 1.0)
    rows, rhs = [], []
    for node in range(3):
        z = reach * math.cos((2 * node + 1) * math.pi / 14)
        g = math.log((1.0 + z) / (1.0 - z)) / z
        rows.append([g, -1.0, z * z])
        rhs.append(g * z * z)
    pole2, joint, slope = [
        det3([[rhs[r] if c == col else rows[r][c] for c in range(3)] for r in range(3)]) / det3(rows)
        for col in range(3)
    ]
    spread = joint - slope * pole2
    centre = 1.0 + root2
    terms = [(-root2 * slope / centre, math.log(centre))]
    for z0 in (math.sqrt(pole2), -math.sqrt(pole2)):
        place = 1.0 - root2 * (1.0 + z0) / (1.0 - z0)
        terms.append((-0.25 * spread * (centre - place) / ((1.0 - z0) * place), math.log(place)))
    at_zero = math.log(root2) - reach * (slope + spread / (pole2 - reach * reach))
    return at_zero - sum(w for w, s in terms), terms


def tile_attend_rankgaps_kernel(tc, query, keys_words, keys_scales, margin, steep, offs, out):
    nc = tc.nc
    level, terms = log1p_terms()
    with ExitStack() as ctx:
        keep = ctx.enter_context(tc.tile_pool(name="keep", bufs=1))
        psum = ctx.enter_context(tc.psum_pool(name="psum", bufs=1))

        offsets = keep.tile([P, I // 16], U16, name="offsets")
        store_scales = keep.tile([P, T], U8, name="store_scales", align_bytes=64)
        store_words = keep.tile([P, T], U16, name="store_words", align_bytes=64)
        query_raw = keep.tile([P, PACK, Q], F32, name="query_raw", tag="behind")
        margin_col = keep.tile([P, PACK], F32, name="margin_col")

        nc.vector.memset(store_scales[:].bitcast(I32), 0)
        zeros = keep.tile([P, P], F32, name="zeros", tag="steep_col")
        nc.vector.memset(zeros[:], 0.0)
        ident = keep.tile([P, P], F32, name="ident", tag="query_codes", align_bytes=64)
        nc.gpsimd.affine_select(
            out=ident[:],
            in_=zeros[:],
            compare_op=ALU.not_equal,
            fill=1.0,
            base=0,
            pattern=[[-1, P]],
            channel_multiplier=1,
        )

        nc.sync.dma_start(offsets[:], offs)
        nc.scalar.dma_start(out=store_words[:].bitcast(I32), in_=keys_words[0].bitcast(I32))
        nc.scalar.dma_start(out=query_raw[:], in_=query.rearrange("(p j) q -> p j q", j=PACK))
        nc.sync.dma_start(out=margin_col[:], in_=margin.rearrange("o (p c) -> (o p) c", c=PACK))
        for row in range(4):
            nc.scalar.dma_start(
                out=store_scales[row:P:32, :].bitcast(I32),
                in_=keys_scales[0, row:16:4, :].bitcast(I32),
            )
        steep_col = keep.tile([P, 1], F32, name="steep_col", tag="steep_col")
        nc.sync.dma_start(out=steep_col[:], in_=steep)

        picked_words = keep.tile([P, I], U16, name="picked_words", align_bytes=64)
        nc.vector.tensor_copy(picked_words[:], store_words[:].indirect(offsets[:]))

        query_bf = keep.tile([P, Q, PACK], BF16, name="query_bf", tag="picked_scales1", align_bytes=64)
        nc.scalar.activation(query_bf[:], query_raw[:].rearrange("p j q -> p q j"), ACT.Copy)

        margin_bank = psum.tile([P, PACK, P], F32, name="margin_bank")
        for c in range(PACK):
            nc.tensor.transpose(margin_bank[:, c, :], margin_col[:, c : c + 1].to_broadcast([P, P]), ident[:])
        behind = keep.tile([P, I], F32, name="behind", tag="behind")
        nc.scalar.activation(
            behind[:].rearrange("q (p c) -> q p c", c=PACK),
            margin_bank[:].rearrange("q c p -> q p c"),
            ACT.Copy,
            scale=steep_col[:],
        )
        nc.scalar.activation(behind[:, 0:1], behind[:, 0:1], ACT.Copy, scale=-1.0)

        picked_scales = [
            keep.tile([P, HALF], U8, name=f"picked_scales{half}", tag=f"picked_scales{half}", align_bytes=64)
            for half in range(2)
        ]

        def gather_scales(half):
            cols = slice(half * HALF // 16, (half + 1) * HALF // 16)
            nc.vector.tensor_copy(picked_scales[half][:], store_scales[:].indirect(offsets[:, cols]))

        gather_scales(0)
        query_codes = keep.tile([P, Q], U32, name="query_codes", tag="query_codes", align_bytes=64)
        query_scales = keep.tile([P, Q], U8, name="query_scales", align_bytes=64)
        nc.vector.quantize_mx(
            out=query_codes[:].bitcast(FP8X4),
            scales=query_scales[:],
            in_=query_bf[:].rearrange("p q j -> p (q j)"),
        )
        gather_scales(1)

        banks = []
        for half in range(2):
            bank = psum.tile([P, HALF], F32, name=f"score_bank{half}")
            nc.tensor.matmul_mx(
                out=bank[:],
                lhsT=query_codes[:].bitcast(FP8X4),
                lhsT_scale=query_scales[:],
                rhs=picked_words[:, half * HALF : (half + 1) * HALF].bitcast(FP4X4),
                rhs_scale=picked_scales[half][:],
                start=True,
                stop=True,
            )
            banks.append(bank)

        gap = keep.tile([P, I], F32, name="gap")
        size = keep.tile([P, I], F32, name="size")
        bends = [keep.tile([P, I], F32, name=f"bend{j}") for j in range(3)]
        sums = [keep.tile([P, I], F32, name=f"sum{j}") for j in range(4)]
        chunks = [(0, 256), (256, 512)]

        def shift(lo, hi):
            bank = banks[lo // HALF]
            base = lo // HALF * HALF
            end = min(hi, I - 1)
            nc.vector.scalar_tensor_tensor(
                behind[:, lo + 1 : end + 1], bank[:, lo - base : end - base], steep_col[:],
                behind[:, lo + 1 : end + 1], ALU.mult, ALU.subtract,
            )

        def diff(lo, hi):
            bank = banks[lo // HALF]
            base = lo // HALF * HALF
            nc.vector.scalar_tensor_tensor(
                gap[:, lo:hi], bank[:, lo - base : hi - base], steep_col[:],
                behind[:, lo:hi], ALU.mult, ALU.subtract,
            )

        for lo, hi in chunks:
            shift(lo, hi)
        for lo, hi in chunks:
            diff(lo, hi)
        for lo, hi in chunks:
            nc.scalar.activation(size[:, lo:hi], gap[:, lo:hi], ACT.Abs)
            nc.vector.tensor_scalar(sums[0][:, lo:hi], gap[:, lo:hi], 0.0, level, ALU.max, ALU.add)
        for j, (weight, place) in enumerate(terms):
            for lo, hi in chunks:
                nc.scalar.activation(bends[j][:, lo:hi], size[:, lo:hi], ACT.Tanh, bias=0.5 * place, scale=0.5)
                nc.vector.scalar_tensor_tensor(
                    sums[j + 1][:, lo:hi], bends[j][:, lo:hi], weight, sums[j][:, lo:hi], ALU.mult, ALU.add
                )
        for lo, hi in chunks:
            nc.sync.dma_start(out=out[:, lo:hi], in_=sums[3][:, lo:hi])
